import numpy as np
import ml_dtypes


def mxq(x, axis, fmt="e4m3"):
    dtype, down = {"e4m3": (ml_dtypes.float8_e4m3fn, 7), "e5m2": (ml_dtypes.float8_e5m2, 14)}[fmt]
    v = np.moveaxis(np.asarray(x, np.float32).astype(ml_dtypes.bfloat16).astype(np.float64), axis, -1)
    blocks = v.reshape(v.shape[:-1] + (-1, 32))
    amax = np.abs(blocks).max(-1, keepdims=True)
    byte = np.maximum(np.where(amax > 0, np.frexp(amax)[1] - 1 + 127, 0) - down, 1)
    scale = np.exp2(byte - 127.0)
    codes = (blocks / scale).astype(np.float32).astype(dtype).astype(np.float64)
    return np.moveaxis((codes * scale).reshape(v.shape), -1, axis)


WIDE = False


def mx_kscale(k):
    if not WIDE:
        return np.ones(k)
    levels = np.array([10, -10, 5, -5, 0])
    if k % 512:
        return np.exp2(np.random.permutation(np.resize(levels, k // 32))).repeat(32)
    a = np.empty((k // 512, 16))
    for p in range(k // 512):
        a[p, :8] = np.random.permutation(np.resize(levels, 8))
        for g in range(8):
            far = levels[np.abs(levels - a[p, g]) >= 10]
            a[p, g + 8] = far[np.random.randint(len(far))]
    return np.exp2(a.ravel()).repeat(32)


def f64(x):
    return np.asarray(x).astype(np.float64)


def striped(idx):
    return np.tile(idx.reshape(-1, 16).T, (8, 1)).astype(np.uint16)


def unstriped(offs):
    return offs[:16].T.reshape(-1).astype(np.int64)


def striped8(idx):
    return np.concatenate([x.reshape(-1, 16).T for x in idx]).astype(np.uint16)


def runs(offs, k):
    lists = np.stack([offs[16 * r : 16 * r + 16].T.reshape(-1) for r in range(8)]).astype(np.int64)
    return lists[np.arange(k) % 512 // 64]


def pack_weight(w):
    k, n = w.shape
    w = f64(np.asarray(w, np.float32).astype(ml_dtypes.bfloat16)).reshape(k // 32, 32, n)
    amax = np.abs(w).max(1)
    byte = np.clip(np.where(amax > 0, np.frexp(amax)[1] - 1 + 127 - 7, 1), 1, 254)
    scaled = (w * np.exp2(127.0 - byte)[:, None, :]).reshape(k, n).astype(np.float32)
    words = np.ascontiguousarray(scaled.reshape(k // 512, 128, 4, n).transpose(0, 1, 3, 2)).astype(ml_dtypes.float8_e4m3fn).view(np.uint8)
    return words, np.ascontiguousarray(byte.astype(np.uint8).reshape(k // 512, 16, n))


def unpack_weight(words, scales):
    g, p, n, _ = words.shape
    vals = np.ascontiguousarray(words).view(ml_dtypes.float8_e4m3fn).astype(np.float64) * np.repeat(np.exp2(scales.astype(np.float64) - 127.0), 8, axis=1)[..., None]
    return vals.transpose(0, 1, 3, 2).reshape(g * 512, n)

def planes(y):
    n, m = y.shape
    v = y.astype(np.float32).astype(ml_dtypes.bfloat16).astype(np.float64).reshape(n // 32, 32, m)
    top = np.abs(v).max(1)
    byte = np.clip(np.where(top > 0, np.frexp(top)[1] - 1 + 127 - 7, 1), 1, 254)
    codes = (v * np.exp2(127.0 - byte)[:, None, :]).reshape(n, m).astype(np.float32).astype(ml_dtypes.float8_e4m3fn).view(np.uint8)
    words = codes.reshape(n // 512, 128, 4, m).transpose(0, 1, 3, 2)
    return np.ascontiguousarray(words), np.ascontiguousarray(byte.astype(np.uint8).reshape(n // 512, 16, m))


K, T, S, N, G, H, W = 512, 1024, 256, 512, 2048, 512, 1024


def setup_inputs():
    n = np.random.standard_normal
    s = mx_kscale(K)[:, None]
    u = mx_kscale(K)
    packed_xT = pack_weight(n((K, T)) * s)
    packed_dT = pack_weight(n((K, G)) / s)
    packed_w1 = pack_weight(n((H, N)) / np.sqrt(2 * H) / u[:, None])
    packed_w2 = pack_weight(n((H, N)) / np.sqrt(2 * H) / u[:, None])
    return {
        "x_words": packed_xT[0],
        "x_scales": packed_xT[1],
        "d_words": packed_dT[0],
        "d_scales": packed_dT[1],
        "gn": (np.random.uniform(0.5, 1.5, (H, 1)) * u[:, None]).astype(np.float32),
        "gm": (np.random.uniform(0.5, 1.5, (H, 1)) * u[:, None]).astype(np.float32),
        "w1_words": packed_w1[0],
        "w1_scales": packed_w1[1],
        "w2_words": packed_w2[0],
        "w2_scales": packed_w2[1],
        "offs": striped(np.random.permutation(T)[:S]),
        "k1": striped8(np.random.randint(0, G, (8, H))),
        "two": striped(np.random.permutation(T)[:S]),
        "n1": striped8(np.stack([np.random.permutation(S) for _ in range(8)])),
        "n2": striped8(np.stack([np.random.permutation(S) for _ in range(8)])),
        "n3": striped(np.random.permutation(S)),
        "n4": striped(np.random.permutation(S)),
        "n5": striped(np.random.randint(0, S, W)),
    }


def reference(x_words, x_scales, d_words, d_scales, gn, gm, w1_words, w1_scales, w2_words, w2_scales, offs, k1, two, n1, n2, n3, n4, n5):
    d_k1 = unpack_weight(d_words, d_scales)[np.arange(K)[:, None], runs(k1, K)]
    xq = unpack_weight(x_words, x_scales)[:, unstriped(offs)]
    a = 0.0625 * (d_k1.T @ xq)
    st = a + a[np.arange(H)[:, None], runs(n1, H)]
    z = f64(gn) * (st * (np.tanh(st[np.arange(H)[:, None], runs(n2, H)])))
    x_two = unpack_weight(x_words, x_scales)[:, unstriped(two)]
    b = 0.0625 * (d_k1.T @ x_two)
    st2 = b + 0.5 * b[:, unstriped(n3)]
    z2 = f64(gm) * (st2 - st2[:, unstriped(n4)])
    h = unpack_weight(w1_words, w1_scales).T @ mxq(z, 0, "e4m3") + unpack_weight(w2_words, w2_scales).T @ mxq(z2, 0, "e4m3")
    ex = np.exp(h)
    mb = ex[:, unstriped(n5)]
    ms = mb.reshape(N, S, 4).sum(axis=2)
    out_0 = np.log(ms + ex) - h
    return (out_0,) + planes(out_0)

@@ -1,0 +1,239 @@
+from contextlib import ExitStack
+
+import concourse.mybir as mybir
+
+F32 = mybir.dt.float32
+BF16 = mybir.dt.bfloat16
+I32 = mybir.dt.int32
+U32 = mybir.dt.uint32
+U16 = mybir.dt.uint16
+U8 = mybir.dt.uint8
+FP8X4 = mybir.dt.float8_e4m3fn_x4
+ALU = mybir.AluOpType
+ACT = mybir.ActivationFunctionType
+AXIS = mybir.AxisListType
+
+P = 128
+PACK = 4
+T, S, G, H, N = 1024, 256, 2048, 512, 512
+MEMBERS = 4
+WIDE = 2 * S
+NARROW = S + 16
+CHUNK = 64
+FLOPS = 4 * 2 * 512 * 512 * S
+
+
+def tile_picked_kjhopphopglse_none_po_kernel(
+    tc, x_words, x_scales, d_words, d_scales, gn, gm, w1_words, w1_scales, w2_words, w2_scales,
+    offs, k1, two, n1, n2, n3, n4, n5, out_0, out_1, out_2,
+):
+    nc = tc.nc
+
+    def words_hbm(ap):
+        return ap[0].rearrange("p n t -> p (n t)").bitcast(I32)
+
+    def deal(engine, dst, src, run):
+        engine.tensor_copy(
+            out=dst.rearrange("p (t c i) -> p c t i", t=PACK, i=run),
+            in_=src.rearrange("p (c i t) -> p c t i", t=PACK, i=run),
+        )
+
+    def interleave(dst, src):
+        nc.vector.tensor_copy(
+            out=dst.rearrange("p (c i) t -> p c t i", i=4),
+            in_=src.rearrange("p t (c i) -> p c t i", i=4),
+        )
+
+    with ExitStack() as ctx:
+        lists = ctx.enter_context(tc.tile_pool(name="lists", bufs=1))
+        keep = ctx.enter_context(tc.tile_pool(name="keep", bufs=1))
+        ring = ctx.enter_context(tc.tile_pool(name="ring", bufs=2))
+        psum = ctx.enter_context(tc.psum_pool(name="psum", bufs=1))
+
+        def load_list(name, ap):
+            held = lists.tile(list(ap.shape), U16, name=name)
+            nc.sync.dma_start(held[:], ap)
+            return held
+
+        d_sc = keep.tile([P, G], U8, name="d_sc", align_bytes=64)
+        x_sc = keep.tile([P, T], U8, name="x_sc", align_bytes=64)
+        key_sc = keep.tile([P, H], U8, name="key_sc", align_bytes=64)
+        nc.gpsimd.memset(key_sc[:].bitcast(I32), 0)
+
+        k1_l = load_list("k1_l", k1)
+        nc.sync.dma_start(d_sc[:].bitcast(I32), d_scales[0].bitcast(I32).unsqueeze(1).broadcast_to([16, 8, G // 4]))
+        for q in range(4):
+            rows = x_scales[0].bitcast(I32)[4 * q : 4 * q + 4, :]
+            nc.scalar.dma_start(x_sc[:].bitcast(I32)[32 * q : 32 * q + 32, :], rows.unsqueeze(0).broadcast_to([8, 4, T // 4]))
+        d_w = keep.tile([P, G], U32, name="d_w", align_bytes=64)
+        nc.sync.dma_start(d_w[:].bitcast(I32), words_hbm(d_words))
+        offs_l = load_list("offs_l", offs)
+        x_w = keep.tile([P, T], U32, name="x_w", align_bytes=64)
+        nc.sync.dma_start(x_w[:].bitcast(I32), words_hbm(x_words))
+        two_l = load_list("two_l", two)
+        n1_l = load_list("n1_l", n1)
+        gm_sb = keep.tile([P, PACK], F32, name="gm_sb")
+        nc.gpsimd.dma_start(gm_sb[:], gm.rearrange("(p t) o -> p (t o)", t=PACK))
+        n3_l = load_list("n3_l", n3)
+        n4_l = load_list("n4_l", n4)
+        n2_l = load_list("n2_l", n2)
+        gn_sb = keep.tile([P, PACK], F32, name="gn_sb")
+        nc.gpsimd.dma_start(gn_sb[:], gn.rearrange("(p t) o -> p (t o)", t=PACK))
+        n5_l = load_list("n5_l", n5)
+
+        wide = [keep.tile([P, WIDE], F32, name="wide%d" % t, align_bytes=64) for t in range(PACK)]
+        narrow = [keep.tile([P, NARROW], F32, name="narrow%d" % t, align_bytes=64) for t in range(PACK)]
+        for t in range(PACK):
+            nc.vector.memset(wide[t][:, S:], 0.0)
+            nc.gpsimd.memset(narrow[t][:, S:], 0.0)
+
+        key_sc_got = keep.tile([P, H], U8, name="key_sc_got", align_bytes=64)
+        nc.vector.tensor_copy(key_sc_got[:], d_sc[:].indirect(k1_l[:]))
+        key_sc_dealt = keep.tile([P, H], U8, name="key_sc_dealt", tag="bytes512", align_bytes=64)
+        deal(nc.vector, key_sc_dealt[:], key_sc_got[:], 16)
+        for r in range(4):
+            src = 8 * r
+            nc.scalar.dma_start(key_sc[:].bitcast(I32)[r:P:32, :], key_sc_dealt[:].bitcast(I32)[src:P:32, :])
+
+        key_w_got = keep.tile([P, H], U32, name="key_w_got", tag="words", align_bytes=64)
+        key_w = keep.tile([P, H], U32, name="key_w", align_bytes=64)
+        tok_sc = [keep.tile([P, S], U8, name="tok_sc%d" % u, align_bytes=64) for u in range(2)]
+        tok_w = [keep.tile([P, S], U32, name="tok_w%d" % u, align_bytes=64) for u in range(2)]
+        nc.vector.tensor_copy(tok_sc[0][:], x_sc[:].indirect(offs_l[:]))
+        nc.vector.tensor_copy(key_w_got[:], d_w[:].indirect(k1_l[:]))
+        deal(nc.vector, key_w[:], key_w_got[:], 4)
+        nc.vector.tensor_copy(tok_w[0][:], x_w[:].indirect(offs_l[:]))
+
+        def scores(u):
+            banks = []
+            for t in range(PACK):
+                bank = psum.tile([P, S], F32, name="score%d%d" % (u, t), tag="bank%d%d" % (u, t))
+                cols = slice(P * t, P * (t + 1))
+                nc.tensor.matmul_mx(
+                    out=bank[:], lhsT=key_w[:, cols].bitcast(FP8X4), lhsT_scale=key_sc[:, cols],
+                    rhs=tok_w[u][:].bitcast(FP8X4), rhs_scale=tok_sc[u][:], start=True, stop=True,
+                )
+                banks.append(bank)
+            return banks
+
+        a_banks = scores(0)
+        nc.vector.tensor_copy(tok_sc[1][:], x_sc[:].indirect(two_l[:]))
+        nc.vector.tensor_copy(tok_w[1][:], x_w[:].indirect(two_l[:]))
+        b_banks = scores(1)
+
+        w_raw = keep.tile([P, 2 * N], U32, name="w_raw", tag="words", align_bytes=64)
+        for u, ap in enumerate((w1_words, w2_words)):
+            nc.sync.dma_start(w_raw[:, N * u : N * (u + 1)].bitcast(I32), words_hbm(ap))
+        w_sc_raw = keep.tile([P, N], U8, name="w_sc_raw", tag="bytes512", align_bytes=64)
+        nc.gpsimd.memset(w_sc_raw[:].bitcast(I32), 0)
+        for u, ap in enumerate((w1_scales, w2_scales)):
+            for q in range(4):
+                nc.sync.dma_start(
+                    w_sc_raw[:].bitcast(I32)[32 * q + 4 * u : 32 * q + 4 * u + 4, :], ap[0].bitcast(I32)[4 * q : 4 * q + 4, :]
+                )
+        w_w = [keep.tile([P, N], U32, name="w_w%d" % u, align_bytes=64) for u in range(2)]
+        w_sc = keep.tile([P, N], U8, name="w_sc", align_bytes=64)
+        for u in range(2):
+            deal(nc.gpsimd, w_w[u][:], w_raw[:, N * u : N * (u + 1)], 4)
+        deal(nc.gpsimd, w_sc[:], w_sc_raw[:], 16)
+
+        gm_neg = keep.tile([P, PACK], F32, name="gm_neg")
+        nc.vector.tensor_scalar(gm_neg[:], gm_sb[:], -0.0625, None, ALU.mult)
+
+        a_n1 = keep.tile([P, PACK, S], F32, name="a_n1")
+        st = keep.tile([P, PACK, S], F32, name="st")
+        th_n2 = keep.tile([P, PACK, S], F32, name="th_n2")
+        z = keep.tile([P, PACK, S], F32, name="z")
+        b_n3 = keep.tile([P, PACK, S], F32, name="b_n3")
+        st2_pos = keep.tile([P, PACK, S], F32, name="st2_pos")
+        z2 = keep.tile([P, PACK, S], F32, name="z2")
+
+        def a_step(t):
+            nc.scalar.activation(wide[t][:, :S], a_banks[t][:], ACT.Copy, scale=0.0625)
+            nc.scalar.activation(a_n1[:, t, :], wide[t][:].indirect(n1_l[:]), ACT.Copy)
+            nc.vector.tensor_tensor(st[:, t, :], wide[t][:, :S], a_n1[:, t, :], ALU.add)
+
+        def b_step(t):
+            if t % 2:
+                nc.scalar.activation(narrow[t][:, :S], b_banks[t][:], ACT.Copy, scale=gm_neg[:, t : t + 1])
+            else:
+                nc.vector.tensor_scalar(narrow[t][:, :S], b_banks[t][:], gm_neg[:, t : t + 1], None, ALU.mult)
+            nc.scalar.activation(b_n3[:, t, :], narrow[t][:].indirect(n3_l[:]), ACT.Copy)
+            nc.vector.scalar_tensor_tensor(narrow[t][:, :S], b_n3[:, t, :], 0.5, narrow[t][:, :S], ALU.mult, ALU.add)
+            nc.vector.tensor_scalar(st2_pos[:, t, :], narrow[t][:, :S], -1.0, None, ALU.mult)
+            nc.vector.tensor_tensor(z2[:, t, :], narrow[t][:].indirect(n4_l[:]), st2_pos[:, t, :], ALU.add)
+
+        a_step(0)
+        for t in range(PACK):
+            if t + 1 < PACK:
+                a_step(t + 1)
+            b_step(t)
+
+        def planes(name):
+            rounded = keep.tile([P, S, PACK], BF16, name=name + "_bf", align_bytes=64)
+            codes = keep.tile([P, S], U32, name=name + "_w", align_bytes=64)
+            scales = keep.tile([P, S], U8, name=name + "_sc", align_bytes=64)
+            return rounded, codes, scales
+
+        def quantize(dst, values, cols):
+            rounded, codes, scales = dst
+            interleave(rounded[:, cols, :], values[:, :, cols])
+            nc.vector.quantize_mx(
+                out=codes[:, cols].bitcast(FP8X4), scales=scales[:, cols], in_=rounded[:, cols, :].rearrange("p j t -> p (j t)")
+            )
+
+        z2_q = planes("z2")
+        z_q = planes("z")
+        quantize(z2_q, z2, slice(0, S))
+        for t in range(PACK):
+            nc.scalar.activation(wide[t][:, :S], st[:, t, :], ACT.Tanh)
+        for half in range(2):
+            cols = slice(half * S // 2, (half + 1) * S // 2)
+            for t in range(PACK):
+                nc.scalar.activation(th_n2[:, t, cols], wide[t][:].indirect(n2_l[:, 8 * half : 8 * half + 8]), ACT.Copy)
+                nc.vector.scalar_tensor_tensor(z[:, t, cols], th_n2[:, t, cols], gn_sb[:, t : t + 1], st[:, t, cols], ALU.mult, ALU.mult)
+            quantize(z_q, z, cols)
+
+        h_banks = [psum.tile([P, S], F32, name="h%d" % t, tag="bank0%d" % t) for t in range(PACK)]
+        for u, (rounded, codes, scales) in ((1, z2_q), (0, z_q)):
+            for t in range(PACK):
+                cols = slice(P * t, P * (t + 1))
+                nc.tensor.matmul_mx(
+                    out=h_banks[t][:], lhsT=w_w[u][:, cols].bitcast(FP8X4), lhsT_scale=w_sc[4 * u :, cols],
+                    rhs=codes[:].bitcast(FP8X4), rhs_scale=scales[:], start=(u == 1), stop=(u == 0),
+                )
+        h = keep.tile([P, PACK, S], F32, name="h")
+        ex = keep.tile([P, PACK, S], F32, name="ex")
+        for t in range(PACK):
+            nc.scalar.activation(narrow[t][:, :S], h_banks[t][:], ACT.Exp)
+            nc.vector.tensor_copy(h[:, t, :], h_banks[t][:])
+            nc.vector.tensor_copy(ex[:, t, :], narrow[t][:, :S])
+
+        out_sc = keep.tile([P, S], U8, name="out_sc", align_bytes=64)
+        out_view = out_0.rearrange("(p t) j -> p t j", t=PACK)
+        out_words = words_hbm(out_1)
+        span = CHUNK * MEMBERS // 16
+        for c in range(S // CHUNK):
+            cols = slice(CHUNK * c, CHUNK * (c + 1))
+            ms = ring.tile([P, PACK, CHUNK], F32, name="ms")
+            for t in range(PACK):
+                mb = ring.tile([P, CHUNK, MEMBERS], F32, name="mb", bufs=4)
+                nc.scalar.activation(
+                    mb[:].rearrange("p j m -> p (j m)"), narrow[t][:].indirect(n5_l[:, span * c : span * (c + 1)]), ACT.Copy
+                )
+                nc.vector.tensor_reduce(ms[:, t, :], mb[:], AXIS.X, ALU.add)
+            total = ring.tile([P, PACK, CHUNK], F32, name="total")
+            nc.vector.tensor_tensor(total[:], ms[:], ex[:, :, cols], ALU.add)
+            logs = ring.tile([P, PACK, CHUNK], F32, name="logs")
+            nc.scalar.activation(logs[:], total[:], ACT.Ln)
+            res = ring.tile([P, PACK, CHUNK], F32, name="res", bufs=4)
+            nc.vector.tensor_tensor(res[:], logs[:], h[:, :, cols], ALU.subtract)
+            nc.sync.dma_start(out_view[:, :, cols], res[:])
+            res_bf = ring.tile([P, CHUNK, PACK], BF16, name="res_bf", align_bytes=64)
+            interleave(res_bf[:], res[:])
+            out_w = ring.tile([P, CHUNK], U32, name="out_w", bufs=4, align_bytes=64)
+            nc.vector.quantize_mx(out=out_w[:].bitcast(FP8X4), scales=out_sc[:, cols], in_=res_bf[:].rearrange("p j t -> p (j t)"))
+            nc.sync.dma_start(out_words[:, cols], out_w[:].bitcast(I32))
+        for q in range(4):
+            queue = nc.scalar if q % 2 else nc.sync
+            queue.dma_start(out_2[0].bitcast(I32)[4 * q : 4 * q + 4, :], out_sc[:].bitcast(I32)[32 * q : 32 * q + 4, :])

@@ -19,6 +19,7 @@ T, S, G, H, N = 1024, 256, 2048, 512, 512
 MEMBERS = 4
 WIDE = 2 * S
 NARROW = S + 16
+ROOMY = S + 96
 CHUNK = 64
 FLOPS = 4 * 2 * 512 * 512 * S
 
@@ -33,7 +34,7 @@ def tile_picked_kjhopphopglse_none_po_kernel(
         return ap[0].rearrange("p n t -> p (n t)").bitcast(I32)
 
     def deal(engine, dst, src, run):
-        engine.tensor_copy(
+        engine(
             out=dst.rearrange("p (t c i) -> p c t i", t=PACK, i=run),
             in_=src.rearrange("p (c i t) -> p c t i", t=PACK, i=run),
         )
@@ -66,17 +67,17 @@ def tile_picked_kjhopphopglse_none_po_kernel(
             rows = x_scales[0].bitcast(I32)[4 * q : 4 * q + 4, :]
             nc.scalar.dma_start(x_sc[:].bitcast(I32)[32 * q : 32 * q + 32, :], rows.unsqueeze(0).broadcast_to([8, 4, T // 4]))
         d_w = keep.tile([P, G], U32, name="d_w", align_bytes=64)
-        nc.sync.dma_start(d_w[:].bitcast(I32), words_hbm(d_words))
         offs_l = load_list("offs_l", offs)
-        x_w = keep.tile([P, T], U32, name="x_w", align_bytes=64)
-        nc.sync.dma_start(x_w[:].bitcast(I32), words_hbm(x_words))
+        nc.sync.dma_start(d_w[:].bitcast(I32), words_hbm(d_words))
         two_l = load_list("two_l", two)
         n1_l = load_list("n1_l", n1)
+        n3_l = load_list("n3_l", n3)
         gm_sb = keep.tile([P, PACK], F32, name="gm_sb")
         nc.gpsimd.dma_start(gm_sb[:], gm.rearrange("(p t) o -> p (t o)", t=PACK))
-        n3_l = load_list("n3_l", n3)
         n4_l = load_list("n4_l", n4)
         n2_l = load_list("n2_l", n2)
+        x_w = keep.tile([P, T], U32, name="x_w", align_bytes=64)
+        nc.sync.dma_start(x_w[:].bitcast(I32), words_hbm(x_words))
         gn_sb = keep.tile([P, PACK], F32, name="gn_sb")
         nc.gpsimd.dma_start(gn_sb[:], gn.rearrange("(p t) o -> p (t o)", t=PACK))
         n5_l = load_list("n5_l", n5)
@@ -90,7 +91,7 @@ def tile_picked_kjhopphopglse_none_po_kernel(
         key_sc_got = keep.tile([P, H], U8, name="key_sc_got", align_bytes=64)
         nc.vector.tensor_copy(key_sc_got[:], d_sc[:].indirect(k1_l[:]))
         key_sc_dealt = keep.tile([P, H], U8, name="key_sc_dealt", tag="bytes512", align_bytes=64)
-        deal(nc.vector, key_sc_dealt[:], key_sc_got[:], 16)
+        deal(nc.vector.tensor_copy, key_sc_dealt[:], key_sc_got[:], 16)
         for r in range(4):
             src = 8 * r
             nc.scalar.dma_start(key_sc[:].bitcast(I32)[r:P:32, :], key_sc_dealt[:].bitcast(I32)[src:P:32, :])
@@ -101,7 +102,7 @@ def tile_picked_kjhopphopglse_none_po_kernel(
         tok_w = [keep.tile([P, S], U32, name="tok_w%d" % u, align_bytes=64) for u in range(2)]
         nc.vector.tensor_copy(tok_sc[0][:], x_sc[:].indirect(offs_l[:]))
         nc.vector.tensor_copy(key_w_got[:], d_w[:].indirect(k1_l[:]))
-        deal(nc.vector, key_w[:], key_w_got[:], 4)
+        deal(nc.vector.tensor_copy, key_w[:], key_w_got[:], 4)
         nc.vector.tensor_copy(tok_w[0][:], x_w[:].indirect(offs_l[:]))
 
         def scores(u):
@@ -131,43 +132,51 @@ def tile_picked_kjhopphopglse_none_po_kernel(
                 nc.sync.dma_start(
                     w_sc_raw[:].bitcast(I32)[32 * q + 4 * u : 32 * q + 4 * u + 4, :], ap[0].bitcast(I32)[4 * q : 4 * q + 4, :]
                 )
-        w_w = [keep.tile([P, N], U32, name="w_w%d" % u, align_bytes=64) for u in range(2)]
-        w_sc = keep.tile([P, N], U8, name="w_sc", align_bytes=64)
-        for u in range(2):
-            deal(nc.gpsimd, w_w[u][:], w_raw[:, N * u : N * (u + 1)], 4)
-        deal(nc.gpsimd, w_sc[:], w_sc_raw[:], 16)
 
-        gm_neg = keep.tile([P, PACK], F32, name="gm_neg")
-        nc.vector.tensor_scalar(gm_neg[:], gm_sb[:], -0.0625, None, ALU.mult)
+        gm_16 = keep.tile([P, PACK], F32, name="gm_16", tag="gm_st")
+        gm_16_late = keep.tile([P, PACK], F32, name="gm_16_late")
+        gn_16 = keep.tile([P, PACK], F32, name="gn_16")
+        gn_safe = keep.tile([P, PACK], F32, name="gn_safe")
+        gn_inv = keep.tile([P, PACK], F32, name="gn_inv")
+        nc.vector.tensor_scalar(gm_16[:], gm_sb[:], 0.0625, None, ALU.mult)
+        nc.vector.tensor_scalar(gm_16_late[:], gm_sb[:], 0.0625, None, ALU.mult)
+        nc.vector.tensor_scalar(gn_16[:], gn_sb[:], 0.0625, None, ALU.mult)
+        nc.vector.scalar_tensor_tensor(gn_safe[:], gn_sb[:], 0.0, gn_sb[:], ALU.is_equal, ALU.add)
+        nc.vector.reciprocal(gn_inv[:], gn_safe[:])
 
-        a_n1 = keep.tile([P, PACK, S], F32, name="a_n1")
-        st = keep.tile([P, PACK, S], F32, name="st")
+        a_n1 = keep.tile([P, PACK, S], F32, name="a_n1", tag="early", align_bytes=64)
         th_n2 = keep.tile([P, PACK, S], F32, name="th_n2")
-        z = keep.tile([P, PACK, S], F32, name="z")
-        b_n3 = keep.tile([P, PACK, S], F32, name="b_n3")
-        st2_pos = keep.tile([P, PACK, S], F32, name="st2_pos")
-        z2 = keep.tile([P, PACK, S], F32, name="z2")
+        b_n3 = keep.tile([P, PACK, S], F32, name="b_n3", tag="early2", align_bytes=64)
+        st2 = keep.tile([P, PACK, ROOMY], F32, name="st2", align_bytes=64)
+        st2_n4 = keep.tile([P, PACK, S], F32, name="st2_n4")
+        nc.gpsimd.memset(st2[:, :, S:], 0.0)
 
         def a_step(t):
-            nc.scalar.activation(wide[t][:, :S], a_banks[t][:], ACT.Copy, scale=0.0625)
+            nc.scalar.activation(wide[t][:, :S], a_banks[t][:], ACT.Copy, scale=gn_16[:, t : t + 1])
             nc.scalar.activation(a_n1[:, t, :], wide[t][:].indirect(n1_l[:]), ACT.Copy)
             nc.vector.tensor_tensor(st[:, t, :], wide[t][:, :S], a_n1[:, t, :], ALU.add)
 
         def b_step(t):
-            if t % 2:
-                nc.scalar.activation(narrow[t][:, :S], b_banks[t][:], ACT.Copy, scale=gm_neg[:, t : t + 1])
-            else:
-                nc.vector.tensor_scalar(narrow[t][:, :S], b_banks[t][:], gm_neg[:, t : t + 1], None, ALU.mult)
+            if t >= 2:
+                nc.scalar.activation(narrow[t][:, :S], b_banks[t][:], ACT.Copy, scale=gm_16_late[:, t : t + 1])
             nc.scalar.activation(b_n3[:, t, :], narrow[t][:].indirect(n3_l[:]), ACT.Copy)
-            nc.vector.scalar_tensor_tensor(narrow[t][:, :S], b_n3[:, t, :], 0.5, narrow[t][:, :S], ALU.mult, ALU.add)
-            nc.vector.tensor_scalar(st2_pos[:, t, :], narrow[t][:, :S], -1.0, None, ALU.mult)
-            nc.vector.tensor_tensor(z2[:, t, :], narrow[t][:].indirect(n4_l[:]), st2_pos[:, t, :], ALU.add)
+            nc.vector.scalar_tensor_tensor(st2[:, t, :S], b_n3[:, t, :], 0.5, narrow[t][:, :S], ALU.mult, ALU.add)
+            nc.vector.tensor_copy(st2_n4[:, t, :], st2[:, t, :].indirect(n4_l[:]))
 
-        a_step(0)
-        for t in range(PACK):
-            if t + 1 < PACK:
-                a_step(t + 1)
-            b_step(t)
+        for t in range(2):
+            nc.vector.tensor_scalar(narrow[t][:, :S], b_banks[t][:], gm_16[:, t : t + 1], None, ALU.mult)
+        st = keep.tile([P, PACK, S], F32, name="st", tag="gm_st")
+        for pair in range(2):
+            if pair == 0:
+                a_step(0)
+                a_step(1)
+                b_step(0)
+                b_step(1)
+            else:
+                a_step(2)
+                b_step(2)
+                a_step(3)
+                b_step(3)
 
         def planes(name):
             rounded = keep.tile([P, S, PACK], BF16, name=name + "_bf", align_bytes=64)
@@ -175,65 +184,77 @@ def tile_picked_kjhopphopglse_none_po_kernel(
             scales = keep.tile([P, S], U8, name=name + "_sc", align_bytes=64)
             return rounded, codes, scales
 
-        def quantize(dst, values, cols):
+        def combine_and_quantize(dst, left, right, op, cols):
             rounded, codes, scales = dst
-            interleave(rounded[:, cols, :], values[:, :, cols])
+            nc.vector.tensor_tensor(
+                rounded[:, cols, :].rearrange("p (c i) t -> p c t i", i=4),
+                left[:, :, cols].rearrange("p t (c i) -> p c t i", i=4),
+                right[:, :, cols].rearrange("p t (c i) -> p c t i", i=4),
+                op,
+            )
             nc.vector.quantize_mx(
                 out=codes[:, cols].bitcast(FP8X4), scales=scales[:, cols], in_=rounded[:, cols, :].rearrange("p j t -> p (j t)")
             )
 
         z2_q = planes("z2")
         z_q = planes("z")
-        quantize(z2_q, z2, slice(0, S))
+        combine_and_quantize(z2_q, st2, st2_n4, ALU.subtract, slice(0, S))
+        w_sc = keep.tile([P, N], U8, name="w_sc", tag="early", align_bytes=64)
+        deal(nc.vector.tensor_copy, w_sc[:], w_sc_raw[:], 16)
+        w_w = keep.tile([P, 2, N], U32, name="w_w", tag="early2", align_bytes=64)
+        for u in range(2):
+            deal(nc.vector.tensor_copy, w_w[:, u, :], w_raw[:, N * u : N * (u + 1)], 4)
         for t in range(PACK):
-            nc.scalar.activation(wide[t][:, :S], st[:, t, :], ACT.Tanh)
-        for half in range(2):
-            cols = slice(half * S // 2, (half + 1) * S // 2)
+            nc.scalar.activation(wide[t][:, :S], st[:, t, :], ACT.Tanh, scale=gn_inv[:, t : t + 1])
+        halves = [slice(half * S // 2, (half + 1) * S // 2) for half in range(2)]
+        for half, cols in enumerate(halves):
             for t in range(PACK):
                 nc.scalar.activation(th_n2[:, t, cols], wide[t][:].indirect(n2_l[:, 8 * half : 8 * half + 8]), ACT.Copy)
-                nc.vector.scalar_tensor_tensor(z[:, t, cols], th_n2[:, t, cols], gn_sb[:, t : t + 1], st[:, t, cols], ALU.mult, ALU.mult)
-            quantize(z_q, z, cols)
+            combine_and_quantize(z_q, st, th_n2, ALU.mult, cols)
 
-        h_banks = [psum.tile([P, S], F32, name="h%d" % t, tag="bank0%d" % t) for t in range(PACK)]
-        for u, (rounded, codes, scales) in ((1, z2_q), (0, z_q)):
-            for t in range(PACK):
-                cols = slice(P * t, P * (t + 1))
-                nc.tensor.matmul_mx(
-                    out=h_banks[t][:], lhsT=w_w[u][:, cols].bitcast(FP8X4), lhsT_scale=w_sc[4 * u :, cols],
-                    rhs=codes[:].bitcast(FP8X4), rhs_scale=scales[:], start=(u == 1), stop=(u == 0),
-                )
         h = keep.tile([P, PACK, S], F32, name="h")
         ex = keep.tile([P, PACK, S], F32, name="ex")
+        for half, cols in enumerate(halves):
+            h_banks = [psum.tile([P, S // 2], F32, name="h%d%d" % (half, t), tag="bank%d%d" % (1 - half, t)) for t in range(PACK)]
+            for u, (rounded, codes, scales) in ((1, z2_q), (0, z_q)):
+                for t in range(PACK):
+                    rows = slice(P * t, P * (t + 1))
+                    nc.tensor.matmul_mx(
+                        out=h_banks[t][:], lhsT=w_w[:, u, rows].bitcast(FP8X4), lhsT_scale=w_sc[4 * u :, rows],
+                        rhs=codes[:, cols].bitcast(FP8X4), rhs_scale=scales[:, cols], start=(u == 1), stop=(u == 0),
+                    )
+            for t in range(PACK):
+                nc.scalar.activation(narrow[t][:, cols], h_banks[t][:], ACT.Exp)
+                nc.vector.tensor_copy(h[:, t, cols], h_banks[t][:])
         for t in range(PACK):
-            nc.scalar.activation(narrow[t][:, :S], h_banks[t][:], ACT.Exp)
-            nc.vector.tensor_copy(h[:, t, :], h_banks[t][:])
             nc.vector.tensor_copy(ex[:, t, :], narrow[t][:, :S])
 
         out_sc = keep.tile([P, S], U8, name="out_sc", align_bytes=64)
         out_view = out_0.rearrange("(p t) j -> p t j", t=PACK)
         out_words = words_hbm(out_1)
-        span = CHUNK * MEMBERS // 16
         for c in range(S // CHUNK):
-            cols = slice(CHUNK * c, CHUNK * (c + 1))
-            ms = ring.tile([P, PACK, CHUNK], F32, name="ms")
-            for t in range(PACK):
-                mb = ring.tile([P, CHUNK, MEMBERS], F32, name="mb", bufs=4)
-                nc.scalar.activation(
-                    mb[:].rearrange("p j m -> p (j m)"), narrow[t][:].indirect(n5_l[:, span * c : span * (c + 1)]), ACT.Copy
-                )
-                nc.vector.tensor_reduce(ms[:, t, :], mb[:], AXIS.X, ALU.add)
-            total = ring.tile([P, PACK, CHUNK], F32, name="total")
-            nc.vector.tensor_tensor(total[:], ms[:], ex[:, :, cols], ALU.add)
-            logs = ring.tile([P, PACK, CHUNK], F32, name="logs")
-            nc.scalar.activation(logs[:], total[:], ACT.Ln)
-            res = ring.tile([P, PACK, CHUNK], F32, name="res", bufs=4)
-            nc.vector.tensor_tensor(res[:], logs[:], h[:, :, cols], ALU.subtract)
-            nc.sync.dma_start(out_view[:, :, cols], res[:])
+            chunk = slice(CHUNK * c, CHUNK * (c + 1))
             res_bf = ring.tile([P, CHUNK, PACK], BF16, name="res_bf", align_bytes=64)
-            interleave(res_bf[:], res[:])
+            width = CHUNK // 2 if c == S // CHUNK - 1 else CHUNK
+            for start in range(chunk.start, chunk.stop, width):
+                cols = slice(start, start + width)
+                entries = slice(start * MEMBERS // 16, (start + width) * MEMBERS // 16)
+                ms = ring.tile([P, PACK, width], F32, name="ms")
+                for t in range(PACK):
+                    mb = ring.tile([P, width, MEMBERS], F32, name="mb", bufs=8)
+                    nc.scalar.activation(mb[:].rearrange("p j m -> p (j m)"), narrow[t][:].indirect(n5_l[:, entries]), ACT.Copy)
+                    nc.vector.tensor_reduce(ms[:, t, :], mb[:], AXIS.X, ALU.add)
+                total = ring.tile([P, PACK, width], F32, name="total")
+                nc.vector.tensor_tensor(total[:], ms[:], ex[:, :, cols], ALU.add)
+                logs = ring.tile([P, PACK, width], F32, name="logs")
+                nc.scalar.activation(logs[:], total[:], ACT.Ln)
+                res = ring.tile([P, PACK, width], F32, name="res", bufs=5)
+                nc.vector.tensor_tensor(res[:], logs[:], h[:, :, cols], ALU.subtract)
+                nc.sync.dma_start(out_view[:, :, cols], res[:])
+                interleave(res_bf[:, start - chunk.start : start - chunk.start + width, :], res[:])
             out_w = ring.tile([P, CHUNK], U32, name="out_w", bufs=4, align_bytes=64)
-            nc.vector.quantize_mx(out=out_w[:].bitcast(FP8X4), scales=out_sc[:, cols], in_=res_bf[:].rearrange("p j t -> p (j t)"))
-            nc.sync.dma_start(out_words[:, cols], out_w[:].bitcast(I32))
+            nc.vector.quantize_mx(out=out_w[:].bitcast(FP8X4), scales=out_sc[:, chunk], in_=res_bf[:].rearrange("p j t -> p (j t)"))
+            nc.sync.dma_start(out_words[:, chunk], out_w[:].bitcast(I32))
         for q in range(4):
             queue = nc.scalar if q % 2 else nc.sync
             queue.dma_start(out_2[0].bitcast(I32)[4 * q : 4 * q + 4, :], out_sc[:].bitcast(I32)[32 * q : 32 * q + 4, :])

@@ -56,30 +56,28 @@ def tile_picked_kjhopphopglse_none_po_kernel(
             nc.sync.dma_start(held[:], ap)
             return held
 
+        gn_sb = keep.tile([P, PACK], F32, name="gn_sb")
+        gm_sb = keep.tile([P, PACK], F32, name="gm_sb")
+        nc.gpsimd.dma_start(gm_sb[:], gm.rearrange("(p t) o -> p (t o)", t=PACK))
+        nc.gpsimd.dma_start(gn_sb[:], gn.rearrange("(p t) o -> p (t o)", t=PACK))
         d_sc = keep.tile([P, G], U8, name="d_sc", align_bytes=64)
         x_sc = keep.tile([P, T], U8, name="x_sc", align_bytes=64)
-        key_sc = keep.tile([P, H], U8, name="key_sc", align_bytes=64)
-        nc.gpsimd.memset(key_sc[:].bitcast(I32), 0)
 
         k1_l = load_list("k1_l", k1)
         nc.sync.dma_start(d_sc[:].bitcast(I32), d_scales[0].bitcast(I32).unsqueeze(1).broadcast_to([16, 8, G // 4]))
+        two_l = load_list("two_l", two)
         for q in range(4):
             rows = x_scales[0].bitcast(I32)[4 * q : 4 * q + 4, :]
-            nc.scalar.dma_start(x_sc[:].bitcast(I32)[32 * q : 32 * q + 32, :], rows.unsqueeze(0).broadcast_to([8, 4, T // 4]))
+            nc.sync.dma_start(x_sc[:].bitcast(I32)[32 * q : 32 * q + 32, :], rows.unsqueeze(0).broadcast_to([8, 4, T // 4]))
         d_w = keep.tile([P, G], U32, name="d_w", align_bytes=64)
-        offs_l = load_list("offs_l", offs)
         nc.sync.dma_start(d_w[:].bitcast(I32), words_hbm(d_words))
-        two_l = load_list("two_l", two)
-        n1_l = load_list("n1_l", n1)
+        offs_l = load_list("offs_l", offs)
         n3_l = load_list("n3_l", n3)
-        gm_sb = keep.tile([P, PACK], F32, name="gm_sb")
-        nc.gpsimd.dma_start(gm_sb[:], gm.rearrange("(p t) o -> p (t o)", t=PACK))
+        n1_l = load_list("n1_l", n1)
         n4_l = load_list("n4_l", n4)
-        n2_l = load_list("n2_l", n2)
         x_w = keep.tile([P, T], U32, name="x_w", align_bytes=64)
         nc.sync.dma_start(x_w[:].bitcast(I32), words_hbm(x_words))
-        gn_sb = keep.tile([P, PACK], F32, name="gn_sb")
-        nc.gpsimd.dma_start(gn_sb[:], gn.rearrange("(p t) o -> p (t o)", t=PACK))
+        n2_l = load_list("n2_l", n2)
         n5_l = load_list("n5_l", n5)
 
         wide = [keep.tile([P, WIDE], F32, name="wide%d" % t, align_bytes=64) for t in range(PACK)]
@@ -88,22 +86,22 @@ def tile_picked_kjhopphopglse_none_po_kernel(
             nc.vector.memset(wide[t][:, S:], 0.0)
             nc.gpsimd.memset(narrow[t][:, S:], 0.0)
 
-        key_sc_got = keep.tile([P, H], U8, name="key_sc_got", align_bytes=64)
+        key_sc_got = keep.tile([P, H], U8, name="key_sc_got", tag="got", align_bytes=64)
         nc.vector.tensor_copy(key_sc_got[:], d_sc[:].indirect(k1_l[:]))
-        key_sc_dealt = keep.tile([P, H], U8, name="key_sc_dealt", tag="bytes512", align_bytes=64)
-        deal(nc.vector.tensor_copy, key_sc_dealt[:], key_sc_got[:], 16)
-        for r in range(4):
+        key_sc = keep.tile([P, H], U8, name="key_sc", align_bytes=64)
+        deal(nc.vector.tensor_copy, key_sc[:], key_sc_got[:], 16)
+        for r in range(1, 4):
             src = 8 * r
-            nc.scalar.dma_start(key_sc[:].bitcast(I32)[r:P:32, :], key_sc_dealt[:].bitcast(I32)[src:P:32, :])
+            nc.scalar.dma_start(key_sc[:].bitcast(I32)[r:P:32, :], key_sc[:].bitcast(I32)[src:P:32, :])
 
-        key_w_got = keep.tile([P, H], U32, name="key_w_got", tag="words", align_bytes=64)
+        key_w_got = keep.tile([P, H], U32, name="key_w_got", align_bytes=64)
         key_w = keep.tile([P, H], U32, name="key_w", align_bytes=64)
-        tok_sc = [keep.tile([P, S], U8, name="tok_sc%d" % u, align_bytes=64) for u in range(2)]
+        tok_sc = keep.tile([P, 2, S], U8, name="tok_sc", tag="got", align_bytes=64)
         tok_w = [keep.tile([P, S], U32, name="tok_w%d" % u, align_bytes=64) for u in range(2)]
-        nc.vector.tensor_copy(tok_sc[0][:], x_sc[:].indirect(offs_l[:]))
+        nc.vector.tensor_copy(tok_sc[:, 1, :], x_sc[:].indirect(two_l[:]))
         nc.vector.tensor_copy(key_w_got[:], d_w[:].indirect(k1_l[:]))
         deal(nc.vector.tensor_copy, key_w[:], key_w_got[:], 4)
-        nc.vector.tensor_copy(tok_w[0][:], x_w[:].indirect(offs_l[:]))
+        nc.vector.tensor_copy(tok_w[1][:], x_w[:].indirect(two_l[:]))
 
         def scores(u):
             banks = []
@@ -112,20 +110,21 @@ def tile_picked_kjhopphopglse_none_po_kernel(
                 cols = slice(P * t, P * (t + 1))
                 nc.tensor.matmul_mx(
                     out=bank[:], lhsT=key_w[:, cols].bitcast(FP8X4), lhsT_scale=key_sc[:, cols],
-                    rhs=tok_w[u][:].bitcast(FP8X4), rhs_scale=tok_sc[u][:], start=True, stop=True,
+                    rhs=tok_w[u][:].bitcast(FP8X4), rhs_scale=tok_sc[:, u, :], start=True, stop=True,
                 )
                 banks.append(bank)
             return banks
 
-        a_banks = scores(0)
-        nc.vector.tensor_copy(tok_sc[1][:], x_sc[:].indirect(two_l[:]))
-        nc.vector.tensor_copy(tok_w[1][:], x_w[:].indirect(two_l[:]))
         b_banks = scores(1)
+        nc.vector.tensor_copy(tok_sc[:, 0, :], x_sc[:].indirect(offs_l[:]))
+        nc.vector.tensor_copy(tok_w[0][:], x_w[:].indirect(offs_l[:]))
+        a_banks = scores(0)
 
-        w_raw = keep.tile([P, 2 * N], U32, name="w_raw", tag="words", align_bytes=64)
+        w_raw = keep.tile([P, 2 * N], U32, name="w_raw", tag="d_sc", align_bytes=64)
         for u, ap in enumerate((w1_words, w2_words)):
             nc.sync.dma_start(w_raw[:, N * u : N * (u + 1)].bitcast(I32), words_hbm(ap))
-        w_sc_raw = keep.tile([P, N], U8, name="w_sc_raw", tag="bytes512", align_bytes=64)
+        w_w = keep.tile([P, 2, N], U32, name="w_w", align_bytes=64)
+        w_sc_raw = keep.tile([P, N], U8, name="w_sc_raw", tag="x_sc", align_bytes=64)
         nc.gpsimd.memset(w_sc_raw[:].bitcast(I32), 0)
         for u, ap in enumerate((w1_scales, w2_scales)):
             for q in range(4):
@@ -133,53 +132,61 @@ def tile_picked_kjhopphopglse_none_po_kernel(
                     w_sc_raw[:].bitcast(I32)[32 * q + 4 * u : 32 * q + 4 * u + 4, :], ap[0].bitcast(I32)[4 * q : 4 * q + 4, :]
                 )
 
-        gm_16 = keep.tile([P, PACK], F32, name="gm_16", tag="gm_st")
-        gm_16_late = keep.tile([P, PACK], F32, name="gm_16_late")
-        gn_16 = keep.tile([P, PACK], F32, name="gn_16")
-        gn_safe = keep.tile([P, PACK], F32, name="gn_safe")
+        gm_16 = keep.tile([P, PACK], F32, name="gm_16")
         gn_inv = keep.tile([P, PACK], F32, name="gn_inv")
-        nc.vector.tensor_scalar(gm_16[:], gm_sb[:], 0.0625, None, ALU.mult)
-        nc.vector.tensor_scalar(gm_16_late[:], gm_sb[:], 0.0625, None, ALU.mult)
-        nc.vector.tensor_scalar(gn_16[:], gn_sb[:], 0.0625, None, ALU.mult)
+        gn_16 = keep.tile([P, PACK], F32, name="gn_16")
+        gn_safe = keep.tile([P, PACK], F32, name="gn_safe", tag="tok_w1", align_bytes=64)
+        nc.scalar.activation(gm_16[:], gm_sb[:], ACT.Copy, scale=0.0625)
+        nc.scalar.activation(gn_16[:], gn_sb[:], ACT.Copy, scale=0.0625)
         nc.vector.scalar_tensor_tensor(gn_safe[:], gn_sb[:], 0.0, gn_sb[:], ALU.is_equal, ALU.add)
         nc.vector.reciprocal(gn_inv[:], gn_safe[:])
 
-        a_n1 = keep.tile([P, PACK, S], F32, name="a_n1", tag="early", align_bytes=64)
+        a_n1 = keep.tile([P, PACK, S], F32, name="a_n1")
         th_n2 = keep.tile([P, PACK, S], F32, name="th_n2")
-        b_n3 = keep.tile([P, PACK, S], F32, name="b_n3", tag="early2", align_bytes=64)
+        b_n3 = keep.tile([P, PACK, S], F32, name="b_n3")
         st2 = keep.tile([P, PACK, ROOMY], F32, name="st2", align_bytes=64)
         st2_n4 = keep.tile([P, PACK, S], F32, name="st2_n4")
         nc.gpsimd.memset(st2[:, :, S:], 0.0)
 
+        def a_copy(t):
+            if t < 2:
+                nc.vector.tensor_scalar(wide[t][:, :S], a_banks[t][:], gn_16[:, t : t + 1], None, ALU.mult)
+            else:
+                nc.scalar.activation(wide[t][:, :S], a_banks[t][:], ACT.Copy, scale=gn_16[:, t : t + 1])
+
         def a_step(t):
-            nc.scalar.activation(wide[t][:, :S], a_banks[t][:], ACT.Copy, scale=gn_16[:, t : t + 1])
             nc.scalar.activation(a_n1[:, t, :], wide[t][:].indirect(n1_l[:]), ACT.Copy)
+
+        def a_sum(t):
             nc.vector.tensor_tensor(st[:, t, :], wide[t][:, :S], a_n1[:, t, :], ALU.add)
 
+        def b_copy(t):
+            nc.scalar.activation(narrow[t][:, :S], b_banks[t][:], ACT.Copy, scale=gm_16[:, t : t + 1])
+
         def b_step(t):
-            if t >= 2:
-                nc.scalar.activation(narrow[t][:, :S], b_banks[t][:], ACT.Copy, scale=gm_16_late[:, t : t + 1])
             nc.scalar.activation(b_n3[:, t, :], narrow[t][:].indirect(n3_l[:]), ACT.Copy)
             nc.vector.scalar_tensor_tensor(st2[:, t, :S], b_n3[:, t, :], 0.5, narrow[t][:, :S], ALU.mult, ALU.add)
+
+        def b_fetch(t):
             nc.vector.tensor_copy(st2_n4[:, t, :], st2[:, t, :].indirect(n4_l[:]))
 
-        for t in range(2):
-            nc.vector.tensor_scalar(narrow[t][:, :S], b_banks[t][:], gm_16[:, t : t + 1], None, ALU.mult)
-        st = keep.tile([P, PACK, S], F32, name="st", tag="gm_st")
-        for pair in range(2):
-            if pair == 0:
-                a_step(0)
-                a_step(1)
-                b_step(0)
-                b_step(1)
-            else:
-                a_step(2)
-                b_step(2)
-                a_step(3)
-                b_step(3)
+        st = keep.tile([P, PACK, S], F32, name="st")
+        w_sc = keep.tile([P, N], U8, name="w_sc", align_bytes=64)
+        b_copy(0)
+        for t in range(PACK):
+            if t + 1 < PACK:
+                b_copy(t + 1)
+            b_step(t)
+            if t < 2:
+                a_copy(t)
+            b_fetch(t)
+        for t in range(PACK):
+            if t in (1, 2):
+                a_copy(t + 1)
+            a_step(t)
 
-        def planes(name):
-            rounded = keep.tile([P, S, PACK], BF16, name=name + "_bf", align_bytes=64)
+        def planes(name, tag):
+            rounded = keep.tile([P, S, PACK], BF16, name=name + "_bf", tag=tag, align_bytes=64)
             codes = keep.tile([P, S], U32, name=name + "_w", align_bytes=64)
             scales = keep.tile([P, S], U8, name=name + "_sc", align_bytes=64)
             return rounded, codes, scales
@@ -196,14 +203,16 @@ def tile_picked_kjhopphopglse_none_po_kernel(
                 out=codes[:, cols].bitcast(FP8X4), scales=scales[:, cols], in_=rounded[:, cols, :].rearrange("p j t -> p (j t)")
             )
 
-        z2_q = planes("z2")
-        z_q = planes("z")
+        z2_q = planes("z2", "z2_bf")
+        a_sum(0)
+        a_sum(1)
         combine_and_quantize(z2_q, st2, st2_n4, ALU.subtract, slice(0, S))
-        w_sc = keep.tile([P, N], U8, name="w_sc", tag="early", align_bytes=64)
+        a_sum(2)
+        a_sum(3)
         deal(nc.vector.tensor_copy, w_sc[:], w_sc_raw[:], 16)
-        w_w = keep.tile([P, 2, N], U32, name="w_w", tag="early2", align_bytes=64)
         for u in range(2):
             deal(nc.vector.tensor_copy, w_w[:, u, :], w_raw[:, N * u : N * (u + 1)], 4)
+        z_q = planes("z", "x_sc")
         for t in range(PACK):
             nc.scalar.activation(wide[t][:, :S], st[:, t, :], ACT.Tanh, scale=gn_inv[:, t : t + 1])
         halves = [slice(half * S // 2, (half + 1) * S // 2) for half in range(2)]
@@ -224,10 +233,10 @@ def tile_picked_kjhopphopglse_none_po_kernel(
                         rhs=codes[:, cols].bitcast(FP8X4), rhs_scale=scales[:, cols], start=(u == 1), stop=(u == 0),
                     )
             for t in range(PACK):
-                nc.scalar.activation(narrow[t][:, cols], h_banks[t][:], ACT.Exp)
+                nc.scalar.activation(wide[t][:, cols], h_banks[t][:], ACT.Exp)
                 nc.vector.tensor_copy(h[:, t, cols], h_banks[t][:])
         for t in range(PACK):
-            nc.vector.tensor_copy(ex[:, t, :], narrow[t][:, :S])
+            nc.vector.tensor_copy(ex[:, t, :], wide[t][:, :S])
 
         out_sc = keep.tile([P, S], U8, name="out_sc", align_bytes=64)
         out_view = out_0.rearrange("(p t) j -> p t j", t=PACK)
@@ -235,14 +244,14 @@ def tile_picked_kjhopphopglse_none_po_kernel(
         for c in range(S // CHUNK):
             chunk = slice(CHUNK * c, CHUNK * (c + 1))
             res_bf = ring.tile([P, CHUNK, PACK], BF16, name="res_bf", align_bytes=64)
-            width = CHUNK // 2 if c == S // CHUNK - 1 else CHUNK
+            width = CHUNK
             for start in range(chunk.start, chunk.stop, width):
                 cols = slice(start, start + width)
                 entries = slice(start * MEMBERS // 16, (start + width) * MEMBERS // 16)
                 ms = ring.tile([P, PACK, width], F32, name="ms")
                 for t in range(PACK):
-                    mb = ring.tile([P, width, MEMBERS], F32, name="mb", bufs=8)
-                    nc.scalar.activation(mb[:].rearrange("p j m -> p (j m)"), narrow[t][:].indirect(n5_l[:, entries]), ACT.Copy)
+                    mb = ring.tile([P, width, MEMBERS], F32, name="mb", bufs=4)
+                    nc.scalar.activation(mb[:].rearrange("p j m -> p (j m)"), wide[t][:].indirect(n5_l[:, entries]), ACT.Copy)
                     nc.vector.tensor_reduce(ms[:, t, :], mb[:], AXIS.X, ALU.add)
                 total = ring.tile([P, PACK, width], F32, name="total")
                 nc.vector.tensor_tensor(total[:], ms[:], ex[:, :, cols], ALU.add)

@@ -15,12 +15,18 @@ AXIS = mybir.AxisListType
 
 P = 128
 PACK = 4
+QUADRANTS = 4
+GROUP = 16
 T, S, G, H, N = 1024, 256, 2048, 512, 512
 MEMBERS = 4
-WIDE = 2 * S
-NARROW = S + 16
-ROOMY = S + 96
+SIXTEENTH = 0.0625
+A_WINDOW = 2 * S
+B_WINDOW = S + 16
+ST2_WINDOW = S + 96
 CHUNK = 64
+A_ON_VECTOR = 2
+A, B = 0, 1
+W1, W2 = 0, 1
 FLOPS = 4 * 2 * 512 * 512 * S
 
 
@@ -33,17 +39,17 @@ def tile_picked_kjhopphopglse_none_po_kernel(
     def words_hbm(ap):
         return ap[0].rearrange("p n t -> p (n t)").bitcast(I32)
 
-    def deal(engine, dst, src, run):
-        engine(
+    def deal(dst, src, run):
+        nc.vector.tensor_copy(
             out=dst.rearrange("p (t c i) -> p c t i", t=PACK, i=run),
             in_=src.rearrange("p (c i t) -> p c t i", t=PACK, i=run),
         )
 
-    def interleave(dst, src):
-        nc.vector.tensor_copy(
-            out=dst.rearrange("p (c i) t -> p c t i", i=4),
-            in_=src.rearrange("p t (c i) -> p c t i", i=4),
-        )
+    def by_row_tile(ap):
+        return ap.rearrange("p t (c i) -> p c t i", i=4)
+
+    def by_column(ap):
+        return ap.rearrange("p (c i) t -> p c t i", i=4)
 
     with ExitStack() as ctx:
         lists = ctx.enter_context(tc.tile_pool(name="lists", bufs=1))
@@ -66,7 +72,7 @@ def tile_picked_kjhopphopglse_none_po_kernel(
         k1_l = load_list("k1_l", k1)
         nc.sync.dma_start(d_sc[:].bitcast(I32), d_scales[0].bitcast(I32).unsqueeze(1).broadcast_to([16, 8, G // 4]))
         two_l = load_list("two_l", two)
-        for q in range(4):
+        for q in range(QUADRANTS):
             rows = x_scales[0].bitcast(I32)[4 * q : 4 * q + 4, :]
             nc.sync.dma_start(x_sc[:].bitcast(I32)[32 * q : 32 * q + 32, :], rows.unsqueeze(0).broadcast_to([8, 4, T // 4]))
         d_w = keep.tile([P, G], U32, name="d_w", align_bytes=64)
@@ -74,60 +80,59 @@ def tile_picked_kjhopphopglse_none_po_kernel(
         offs_l = load_list("offs_l", offs)
         n3_l = load_list("n3_l", n3)
         n1_l = load_list("n1_l", n1)
-        n4_l = load_list("n4_l", n4)
         x_w = keep.tile([P, T], U32, name="x_w", align_bytes=64)
         nc.sync.dma_start(x_w[:].bitcast(I32), words_hbm(x_words))
+        n4_l = load_list("n4_l", n4)
         n2_l = load_list("n2_l", n2)
         n5_l = load_list("n5_l", n5)
 
-        wide = [keep.tile([P, WIDE], F32, name="wide%d" % t, align_bytes=64) for t in range(PACK)]
-        narrow = [keep.tile([P, NARROW], F32, name="narrow%d" % t, align_bytes=64) for t in range(PACK)]
+        a_win = [keep.tile([P, A_WINDOW], F32, name="a_win%d" % t, align_bytes=64) for t in range(PACK)]
+        b_win = [keep.tile([P, B_WINDOW], F32, name="b_win%d" % t, align_bytes=64) for t in range(PACK)]
         for t in range(PACK):
-            nc.vector.memset(wide[t][:, S:], 0.0)
-            nc.gpsimd.memset(narrow[t][:, S:], 0.0)
+            nc.vector.memset(a_win[t][:, S:], 0.0)
+            nc.gpsimd.memset(b_win[t][:, S:], 0.0)
 
-        key_sc_got = keep.tile([P, H], U8, name="key_sc_got", tag="got", align_bytes=64)
+        key_sc_got = keep.tile([P, H], U8, name="key_sc_got", tag="got_bytes", align_bytes=64)
         nc.vector.tensor_copy(key_sc_got[:], d_sc[:].indirect(k1_l[:]))
         key_sc = keep.tile([P, H], U8, name="key_sc", align_bytes=64)
-        deal(nc.vector.tensor_copy, key_sc[:], key_sc_got[:], 16)
+        deal(key_sc[:], key_sc_got[:], 16)
         for r in range(1, 4):
-            src = 8 * r
-            nc.scalar.dma_start(key_sc[:].bitcast(I32)[r:P:32, :], key_sc[:].bitcast(I32)[src:P:32, :])
+            nc.scalar.dma_start(key_sc[:].bitcast(I32)[r:P:32, :], key_sc[:].bitcast(I32)[8 * r : P : 32, :])
 
         key_w_got = keep.tile([P, H], U32, name="key_w_got", align_bytes=64)
         key_w = keep.tile([P, H], U32, name="key_w", align_bytes=64)
-        tok_sc = keep.tile([P, 2, S], U8, name="tok_sc", tag="got", align_bytes=64)
-        tok_w = [keep.tile([P, S], U32, name="tok_w%d" % u, align_bytes=64) for u in range(2)]
-        nc.vector.tensor_copy(tok_sc[:, 1, :], x_sc[:].indirect(two_l[:]))
+        tok_sc = keep.tile([P, 2, S], U8, name="tok_sc", tag="got_bytes", align_bytes=64)
+        tok_w = [keep.tile([P, S], U32, name="tok_w%d" % u, align_bytes=64) for u in (A, B)]
+        nc.vector.tensor_copy(tok_sc[:, B, :], x_sc[:].indirect(two_l[:]))
         nc.vector.tensor_copy(key_w_got[:], d_w[:].indirect(k1_l[:]))
-        deal(nc.vector.tensor_copy, key_w[:], key_w_got[:], 4)
-        nc.vector.tensor_copy(tok_w[1][:], x_w[:].indirect(two_l[:]))
+        deal(key_w[:], key_w_got[:], 4)
+        nc.vector.tensor_copy(tok_w[B][:], x_w[:].indirect(two_l[:]))
 
         def scores(u):
             banks = []
             for t in range(PACK):
                 bank = psum.tile([P, S], F32, name="score%d%d" % (u, t), tag="bank%d%d" % (u, t))
-                cols = slice(P * t, P * (t + 1))
+                keys = slice(P * t, P * (t + 1))
                 nc.tensor.matmul_mx(
-                    out=bank[:], lhsT=key_w[:, cols].bitcast(FP8X4), lhsT_scale=key_sc[:, cols],
+                    out=bank[:], lhsT=key_w[:, keys].bitcast(FP8X4), lhsT_scale=key_sc[:, keys],
                     rhs=tok_w[u][:].bitcast(FP8X4), rhs_scale=tok_sc[:, u, :], start=True, stop=True,
                 )
                 banks.append(bank)
             return banks
 
-        b_banks = scores(1)
-        nc.vector.tensor_copy(tok_sc[:, 0, :], x_sc[:].indirect(offs_l[:]))
-        nc.vector.tensor_copy(tok_w[0][:], x_w[:].indirect(offs_l[:]))
-        a_banks = scores(0)
+        b_banks = scores(B)
+        nc.vector.tensor_copy(tok_sc[:, A, :], x_sc[:].indirect(offs_l[:]))
+        nc.vector.tensor_copy(tok_w[A][:], x_w[:].indirect(offs_l[:]))
+        a_banks = scores(A)
 
-        w_raw = keep.tile([P, 2 * N], U32, name="w_raw", tag="d_sc", align_bytes=64)
-        for u, ap in enumerate((w1_words, w2_words)):
+        w_raw = keep.tile([P, 2 * N], U32, name="w_raw", tag="d_w", align_bytes=64)
+        for u, ap in ((W1, w1_words), (W2, w2_words)):
             nc.sync.dma_start(w_raw[:, N * u : N * (u + 1)].bitcast(I32), words_hbm(ap))
         w_w = keep.tile([P, 2, N], U32, name="w_w", align_bytes=64)
         w_sc_raw = keep.tile([P, N], U8, name="w_sc_raw", tag="x_sc", align_bytes=64)
         nc.gpsimd.memset(w_sc_raw[:].bitcast(I32), 0)
-        for u, ap in enumerate((w1_scales, w2_scales)):
-            for q in range(4):
+        for u, ap in ((W1, w1_scales), (W2, w2_scales)):
+            for q in range(QUADRANTS):
                 nc.sync.dma_start(
                     w_sc_raw[:].bitcast(I32)[32 * q + 4 * u : 32 * q + 4 * u + 4, :], ap[0].bitcast(I32)[4 * q : 4 * q + 4, :]
                 )
@@ -135,57 +140,48 @@ def tile_picked_kjhopphopglse_none_po_kernel(
         gm_16 = keep.tile([P, PACK], F32, name="gm_16")
         gn_inv = keep.tile([P, PACK], F32, name="gn_inv")
         gn_16 = keep.tile([P, PACK], F32, name="gn_16")
-        gn_safe = keep.tile([P, PACK], F32, name="gn_safe", tag="tok_w1", align_bytes=64)
-        nc.scalar.activation(gm_16[:], gm_sb[:], ACT.Copy, scale=0.0625)
-        nc.scalar.activation(gn_16[:], gn_sb[:], ACT.Copy, scale=0.0625)
+        gn_safe = keep.tile([P, PACK], F32, name="gn_safe", tag="tok_w%d" % B, align_bytes=64)
+        nc.scalar.activation(gm_16[:], gm_sb[:], ACT.Copy, scale=SIXTEENTH)
+        nc.scalar.activation(gn_16[:], gn_sb[:], ACT.Copy, scale=SIXTEENTH)
         nc.vector.scalar_tensor_tensor(gn_safe[:], gn_sb[:], 0.0, gn_sb[:], ALU.is_equal, ALU.add)
         nc.vector.reciprocal(gn_inv[:], gn_safe[:])
 
         a_n1 = keep.tile([P, PACK, S], F32, name="a_n1")
-        th_n2 = keep.tile([P, PACK, S], F32, name="th_n2")
+        tanh_n2 = keep.tile([P, PACK, S], F32, name="tanh_n2")
         b_n3 = keep.tile([P, PACK, S], F32, name="b_n3")
-        st2 = keep.tile([P, PACK, ROOMY], F32, name="st2", align_bytes=64)
+        st2 = keep.tile([P, PACK, ST2_WINDOW], F32, name="st2", align_bytes=64)
         st2_n4 = keep.tile([P, PACK, S], F32, name="st2_n4")
         nc.gpsimd.memset(st2[:, :, S:], 0.0)
 
-        def a_copy(t):
-            if t < 2:
-                nc.vector.tensor_scalar(wide[t][:, :S], a_banks[t][:], gn_16[:, t : t + 1], None, ALU.mult)
+        def copy_a(t):
+            if t < A_ON_VECTOR:
+                nc.vector.tensor_scalar(a_win[t][:, :S], a_banks[t][:], gn_16[:, t : t + 1], None, ALU.mult)
             else:
-                nc.scalar.activation(wide[t][:, :S], a_banks[t][:], ACT.Copy, scale=gn_16[:, t : t + 1])
+                nc.scalar.activation(a_win[t][:, :S], a_banks[t][:], ACT.Copy, scale=gn_16[:, t : t + 1])
 
-        def a_step(t):
-            nc.scalar.activation(a_n1[:, t, :], wide[t][:].indirect(n1_l[:]), ACT.Copy)
+        def make_st(t):
+            nc.vector.tensor_tensor(st[:, t, :], a_win[t][:, :S], a_n1[:, t, :], ALU.add)
 
-        def a_sum(t):
-            nc.vector.tensor_tensor(st[:, t, :], wide[t][:, :S], a_n1[:, t, :], ALU.add)
-
-        def b_copy(t):
-            nc.scalar.activation(narrow[t][:, :S], b_banks[t][:], ACT.Copy, scale=gm_16[:, t : t + 1])
-
-        def b_step(t):
-            nc.scalar.activation(b_n3[:, t, :], narrow[t][:].indirect(n3_l[:]), ACT.Copy)
-            nc.vector.scalar_tensor_tensor(st2[:, t, :S], b_n3[:, t, :], 0.5, narrow[t][:, :S], ALU.mult, ALU.add)
-
-        def b_fetch(t):
-            nc.vector.tensor_copy(st2_n4[:, t, :], st2[:, t, :].indirect(n4_l[:]))
+        def copy_b(t):
+            nc.scalar.activation(b_win[t][:, :S], b_banks[t][:], ACT.Copy, scale=gm_16[:, t : t + 1])
 
         st = keep.tile([P, PACK, S], F32, name="st")
         w_sc = keep.tile([P, N], U8, name="w_sc", align_bytes=64)
-        b_copy(0)
+        copy_b(0)
         for t in range(PACK):
             if t + 1 < PACK:
-                b_copy(t + 1)
-            b_step(t)
-            if t < 2:
-                a_copy(t)
-            b_fetch(t)
+                copy_b(t + 1)
+            nc.scalar.activation(b_n3[:, t, :], b_win[t][:].indirect(n3_l[:]), ACT.Copy)
+            nc.vector.scalar_tensor_tensor(st2[:, t, :S], b_n3[:, t, :], 0.5, b_win[t][:, :S], ALU.mult, ALU.add)
+            if t < A_ON_VECTOR:
+                copy_a(t)
+            nc.vector.tensor_copy(st2_n4[:, t, :], st2[:, t, :].indirect(n4_l[:]))
         for t in range(PACK):
-            if t in (1, 2):
-                a_copy(t + 1)
-            a_step(t)
+            if A_ON_VECTOR <= t + 1 < PACK:
+                copy_a(t + 1)
+            nc.scalar.activation(a_n1[:, t, :], a_win[t][:].indirect(n1_l[:]), ACT.Copy)
 
-        def planes(name, tag):
+        def mx_tiles(name, tag):
             rounded = keep.tile([P, S, PACK], BF16, name=name + "_bf", tag=tag, align_bytes=64)
             codes = keep.tile([P, S], U32, name=name + "_w", align_bytes=64)
             scales = keep.tile([P, S], U8, name=name + "_sc", align_bytes=64)
@@ -194,76 +190,76 @@ def tile_picked_kjhopphopglse_none_po_kernel(
         def combine_and_quantize(dst, left, right, op, cols):
             rounded, codes, scales = dst
             nc.vector.tensor_tensor(
-                rounded[:, cols, :].rearrange("p (c i) t -> p c t i", i=4),
-                left[:, :, cols].rearrange("p t (c i) -> p c t i", i=4),
-                right[:, :, cols].rearrange("p t (c i) -> p c t i", i=4),
-                op,
+                by_column(rounded[:, cols, :]), by_row_tile(left[:, :, cols]), by_row_tile(right[:, :, cols]), op
             )
             nc.vector.quantize_mx(
                 out=codes[:, cols].bitcast(FP8X4), scales=scales[:, cols], in_=rounded[:, cols, :].rearrange("p j t -> p (j t)")
             )
 
-        z2_q = planes("z2", "z2_bf")
-        a_sum(0)
-        a_sum(1)
-        combine_and_quantize(z2_q, st2, st2_n4, ALU.subtract, slice(0, S))
-        a_sum(2)
-        a_sum(3)
-        deal(nc.vector.tensor_copy, w_sc[:], w_sc_raw[:], 16)
-        for u in range(2):
-            deal(nc.vector.tensor_copy, w_w[:, u, :], w_raw[:, N * u : N * (u + 1)], 4)
-        z_q = planes("z", "x_sc")
+        z2_mx = mx_tiles("z2", "z2_bf")
+        for t in range(PACK // 2):
+            make_st(t)
+        combine_and_quantize(z2_mx, st2, st2_n4, ALU.subtract, slice(0, S))
+        for t in range(PACK // 2, PACK):
+            make_st(t)
+        deal(w_sc[:], w_sc_raw[:], 16)
+        for u in (W1, W2):
+            deal(w_w[:, u, :], w_raw[:, N * u : N * (u + 1)], 4)
+        z_mx = mx_tiles("z", "x_sc")
         for t in range(PACK):
-            nc.scalar.activation(wide[t][:, :S], st[:, t, :], ACT.Tanh, scale=gn_inv[:, t : t + 1])
+            nc.scalar.activation(a_win[t][:, :S], st[:, t, :], ACT.Tanh, scale=gn_inv[:, t : t + 1])
         halves = [slice(half * S // 2, (half + 1) * S // 2) for half in range(2)]
-        for half, cols in enumerate(halves):
+        for cols in halves:
+            entries = slice(cols.start // GROUP, cols.stop // GROUP)
             for t in range(PACK):
-                nc.scalar.activation(th_n2[:, t, cols], wide[t][:].indirect(n2_l[:, 8 * half : 8 * half + 8]), ACT.Copy)
-            combine_and_quantize(z_q, st, th_n2, ALU.mult, cols)
+                nc.scalar.activation(tanh_n2[:, t, cols], a_win[t][:].indirect(n2_l[:, entries]), ACT.Copy)
+            combine_and_quantize(z_mx, st, tanh_n2, ALU.mult, cols)
 
         h = keep.tile([P, PACK, S], F32, name="h")
         ex = keep.tile([P, PACK, S], F32, name="ex")
-        for half, cols in enumerate(halves):
-            h_banks = [psum.tile([P, S // 2], F32, name="h%d%d" % (half, t), tag="bank%d%d" % (1 - half, t)) for t in range(PACK)]
-            for u, (rounded, codes, scales) in ((1, z2_q), (0, z_q)):
+        for left_by, cols in zip((B, A), halves):
+            h_banks = [
+                psum.tile([P, S // 2], F32, name="h%d%d" % (left_by, t), tag="bank%d%d" % (left_by, t)) for t in range(PACK)
+            ]
+            for u, (rounded, codes, scales) in ((W2, z2_mx), (W1, z_mx)):
                 for t in range(PACK):
-                    rows = slice(P * t, P * (t + 1))
+                    outs = slice(P * t, P * (t + 1))
                     nc.tensor.matmul_mx(
-                        out=h_banks[t][:], lhsT=w_w[:, u, rows].bitcast(FP8X4), lhsT_scale=w_sc[4 * u :, rows],
-                        rhs=codes[:, cols].bitcast(FP8X4), rhs_scale=scales[:, cols], start=(u == 1), stop=(u == 0),
+                        out=h_banks[t][:], lhsT=w_w[:, u, outs].bitcast(FP8X4), lhsT_scale=w_sc[4 * u :, outs],
+                        rhs=codes[:, cols].bitcast(FP8X4), rhs_scale=scales[:, cols], start=(u == W2), stop=(u == W1),
                     )
             for t in range(PACK):
-                nc.scalar.activation(wide[t][:, cols], h_banks[t][:], ACT.Exp)
+                nc.scalar.activation(a_win[t][:, cols], h_banks[t][:], ACT.Exp)
                 nc.vector.tensor_copy(h[:, t, cols], h_banks[t][:])
         for t in range(PACK):
-            nc.vector.tensor_copy(ex[:, t, :], wide[t][:, :S])
+            nc.vector.tensor_copy(ex[:, t, :], a_win[t][:, :S])
 
         out_sc = keep.tile([P, S], U8, name="out_sc", align_bytes=64)
-        out_view = out_0.rearrange("(p t) j -> p t j", t=PACK)
+        out_rows = out_0.rearrange("(p t) j -> p t j", t=PACK)
         out_words = words_hbm(out_1)
-        for c in range(S // CHUNK):
-            chunk = slice(CHUNK * c, CHUNK * (c + 1))
-            res_bf = ring.tile([P, CHUNK, PACK], BF16, name="res_bf", align_bytes=64)
-            width = CHUNK
-            for start in range(chunk.start, chunk.stop, width):
-                cols = slice(start, start + width)
-                entries = slice(start * MEMBERS // 16, (start + width) * MEMBERS // 16)
-                ms = ring.tile([P, PACK, width], F32, name="ms")
-                for t in range(PACK):
-                    mb = ring.tile([P, width, MEMBERS], F32, name="mb", bufs=4)
-                    nc.scalar.activation(mb[:].rearrange("p j m -> p (j m)"), wide[t][:].indirect(n5_l[:, entries]), ACT.Copy)
+        chunks = S // CHUNK
+        for c in range(chunks):
+            cols = slice(CHUNK * c, CHUNK * (c + 1))
+            entries = slice(cols.start * MEMBERS // GROUP, cols.stop * MEMBERS // GROUP)
+            ms = ring.tile([P, PACK, CHUNK], F32, name="ms")
+            total = ring.tile([P, PACK, CHUNK], F32, name="total")
+            logs = ring.tile([P, PACK, CHUNK], F32, name="logs")
+            res = ring.tile([P, PACK, CHUNK], F32, name="res", bufs=chunks)
+            parts = (slice(0, PACK - 1), slice(PACK - 1, PACK)) if c == chunks - 1 else (slice(0, PACK),)
+            for part in parts:
+                for t in range(part.start, part.stop):
+                    mb = ring.tile([P, CHUNK, MEMBERS], F32, name="mb", bufs=PACK)
+                    nc.scalar.activation(mb[:].rearrange("p j m -> p (j m)"), a_win[t][:].indirect(n5_l[:, entries]), ACT.Copy)
                     nc.vector.tensor_reduce(ms[:, t, :], mb[:], AXIS.X, ALU.add)
-                total = ring.tile([P, PACK, width], F32, name="total")
-                nc.vector.tensor_tensor(total[:], ms[:], ex[:, :, cols], ALU.add)
-                logs = ring.tile([P, PACK, width], F32, name="logs")
-                nc.scalar.activation(logs[:], total[:], ACT.Ln)
-                res = ring.tile([P, PACK, width], F32, name="res", bufs=5)
-                nc.vector.tensor_tensor(res[:], logs[:], h[:, :, cols], ALU.subtract)
-                nc.sync.dma_start(out_view[:, :, cols], res[:])
-                interleave(res_bf[:, start - chunk.start : start - chunk.start + width, :], res[:])
-            out_w = ring.tile([P, CHUNK], U32, name="out_w", bufs=4, align_bytes=64)
-            nc.vector.quantize_mx(out=out_w[:].bitcast(FP8X4), scales=out_sc[:, chunk], in_=res_bf[:].rearrange("p j t -> p (j t)"))
-            nc.sync.dma_start(out_words[:, chunk], out_w[:].bitcast(I32))
-        for q in range(4):
+                nc.vector.tensor_tensor(total[:, part, :], ms[:, part, :], ex[:, part, cols], ALU.add)
+                nc.scalar.activation(logs[:, part, :], total[:, part, :], ACT.Ln)
+                nc.vector.tensor_tensor(res[:, part, :], logs[:, part, :], h[:, part, cols], ALU.subtract)
+            nc.sync.dma_start(out_rows[:, :, cols], res[:])
+            res_bf = ring.tile([P, CHUNK, PACK], BF16, name="res_bf", align_bytes=64)
+            nc.vector.tensor_copy(out=by_column(res_bf[:]), in_=by_row_tile(res[:]))
+            out_w = ring.tile([P, CHUNK], U32, name="out_w", bufs=chunks, align_bytes=64)
+            nc.vector.quantize_mx(out=out_w[:].bitcast(FP8X4), scales=out_sc[:, cols], in_=res_bf[:].rearrange("p j t -> p (j t)"))
+            nc.sync.dma_start(out_words[:, cols], out_w[:].bitcast(I32))
+        for q in range(QUADRANTS):
             queue = nc.scalar if q % 2 else nc.sync
             queue.dma_start(out_2[0].bitcast(I32)[4 * q : 4 * q + 4, :], out_sc[:].bitcast(I32)[32 * q : 32 * q + 4, :])

from contextlib import ExitStack

import concourse.mybir as mybir

F32 = mybir.dt.float32
BF16 = mybir.dt.bfloat16
I32 = mybir.dt.int32
U32 = mybir.dt.uint32
U16 = mybir.dt.uint16
U8 = mybir.dt.uint8
FP8X4 = mybir.dt.float8_e4m3fn_x4
ALU = mybir.AluOpType
ACT = mybir.ActivationFunctionType
AXIS = mybir.AxisListType

P = 128
PACK = 4
QUADRANTS = 4
GROUP = 16
T, S, G, H, N = 1024, 256, 2048, 512, 512
MEMBERS = 4
SIXTEENTH = 0.0625
A_WINDOW = 2 * S
B_WINDOW = S + 16
ST2_WINDOW = S + 96
CHUNK = 64
A_ON_VECTOR = 2
A, B = 0, 1
W1, W2 = 0, 1
FLOPS = 4 * 2 * 512 * 512 * S


def tile_picked_kjhopphopglse_none_po_kernel(
    tc, x_words, x_scales, d_words, d_scales, gn, gm, w1_words, w1_scales, w2_words, w2_scales,
    offs, k1, two, n1, n2, n3, n4, n5, out_0, out_1, out_2,
):
    nc = tc.nc

    def words_hbm(ap):
        return ap[0].rearrange("p n t -> p (n t)").bitcast(I32)

    def deal(dst, src, run):
        nc.vector.tensor_copy(
            out=dst.rearrange("p (t c i) -> p c t i", t=PACK, i=run),
            in_=src.rearrange("p (c i t) -> p c t i", t=PACK, i=run),
        )

    def by_row_tile(ap):
        return ap.rearrange("p t (c i) -> p c t i", i=4)

    def by_column(ap):
        return ap.rearrange("p (c i) t -> p c t i", i=4)

    with ExitStack() as ctx:
        lists = ctx.enter_context(tc.tile_pool(name="lists", bufs=1))
        keep = ctx.enter_context(tc.tile_pool(name="keep", bufs=1))
        ring = ctx.enter_context(tc.tile_pool(name="ring", bufs=2))
        psum = ctx.enter_context(tc.psum_pool(name="psum", bufs=1))

        def load_list(name, ap):
            held = lists.tile(list(ap.shape), U16, name=name)
            nc.sync.dma_start(held[:], ap)
            return held

        gn_sb = keep.tile([P, PACK], F32, name="gn_sb")
        gm_sb = keep.tile([P, PACK], F32, name="gm_sb")
        nc.gpsimd.dma_start(gm_sb[:], gm.rearrange("(p t) o -> p (t o)", t=PACK))
        nc.gpsimd.dma_start(gn_sb[:], gn.rearrange("(p t) o -> p (t o)", t=PACK))
        d_sc = keep.tile([P, G], U8, name="d_sc", align_bytes=64)
        x_sc = keep.tile([P, T], U8, name="x_sc", align_bytes=64)

        k1_l = load_list("k1_l", k1)
        nc.sync.dma_start(d_sc[:].bitcast(I32), d_scales[0].bitcast(I32).unsqueeze(1).broadcast_to([16, 8, G // 4]))
        two_l = load_list("two_l", two)
        for q in range(QUADRANTS):
            rows = x_scales[0].bitcast(I32)[4 * q : 4 * q + 4, :]
            nc.sync.dma_start(x_sc[:].bitcast(I32)[32 * q : 32 * q + 32, :], rows.unsqueeze(0).broadcast_to([8, 4, T // 4]))
        d_w = keep.tile([P, G], U32, name="d_w", align_bytes=64)
        nc.sync.dma_start(d_w[:].bitcast(I32), words_hbm(d_words))
        offs_l = load_list("offs_l", offs)
        n3_l = load_list("n3_l", n3)
        n1_l = load_list("n1_l", n1)
        x_w = keep.tile([P, T], U32, name="x_w", align_bytes=64)
        nc.sync.dma_start(x_w[:].bitcast(I32), words_hbm(x_words))
        n4_l = load_list("n4_l", n4)
        n2_l = load_list("n2_l", n2)
        n5_l = load_list("n5_l", n5)

        a_win = [keep.tile([P, A_WINDOW], F32, name="a_win%d" % t, align_bytes=64) for t in range(PACK)]
        b_win = [keep.tile([P, B_WINDOW], F32, name="b_win%d" % t, align_bytes=64) for t in range(PACK)]
        for t in range(PACK):
            nc.vector.memset(a_win[t][:, S:], 0.0)
            nc.gpsimd.memset(b_win[t][:, S:], 0.0)

        key_sc_got = keep.tile([P, H], U8, name="key_sc_got", tag="got_bytes", align_bytes=64)
        nc.vector.tensor_copy(key_sc_got[:], d_sc[:].indirect(k1_l[:]))
        key_sc = keep.tile([P, H], U8, name="key_sc", align_bytes=64)
        deal(key_sc[:], key_sc_got[:], 16)
        for r in range(1, 4):
            nc.scalar.dma_start(key_sc[:].bitcast(I32)[r:P:32, :], key_sc[:].bitcast(I32)[8 * r : P : 32, :])

        key_w_got = keep.tile([P, H], U32, name="key_w_got", align_bytes=64)
        key_w = keep.tile([P, H], U32, name="key_w", align_bytes=64)
        tok_sc = keep.tile([P, 2, S], U8, name="tok_sc", tag="got_bytes", align_bytes=64)
        tok_w = [keep.tile([P, S], U32, name="tok_w%d" % u, align_bytes=64) for u in (A, B)]
        nc.vector.tensor_copy(tok_sc[:, B, :], x_sc[:].indirect(two_l[:]))
        nc.vector.tensor_copy(key_w_got[:], d_w[:].indirect(k1_l[:]))
        deal(key_w[:], key_w_got[:], 4)
        nc.vector.tensor_copy(tok_w[B][:], x_w[:].indirect(two_l[:]))

        def scores(u):
            banks = []
            for t in range(PACK):
                bank = psum.tile([P, S], F32, name="score%d%d" % (u, t), tag="bank%d%d" % (u, t))
                keys = slice(P * t, P * (t + 1))
                nc.tensor.matmul_mx(
                    out=bank[:], lhsT=key_w[:, keys].bitcast(FP8X4), lhsT_scale=key_sc[:, keys],
                    rhs=tok_w[u][:].bitcast(FP8X4), rhs_scale=tok_sc[:, u, :], start=True, stop=True,
                )
                banks.append(bank)
            return banks

        b_banks = scores(B)
        nc.vector.tensor_copy(tok_sc[:, A, :], x_sc[:].indirect(offs_l[:]))
        nc.vector.tensor_copy(tok_w[A][:], x_w[:].indirect(offs_l[:]))
        a_banks = scores(A)

        w_raw = keep.tile([P, 2 * N], U32, name="w_raw", tag="d_w", align_bytes=64)
        for u, ap in ((W1, w1_words), (W2, w2_words)):
            nc.sync.dma_start(w_raw[:, N * u : N * (u + 1)].bitcast(I32), words_hbm(ap))
        w_w = keep.tile([P, 2, N], U32, name="w_w", align_bytes=64)
        w_sc_raw = keep.tile([P, N], U8, name="w_sc_raw", tag="x_sc", align_bytes=64)
        nc.gpsimd.memset(w_sc_raw[:].bitcast(I32), 0)
        for u, ap in ((W1, w1_scales), (W2, w2_scales)):
            for q in range(QUADRANTS):
                nc.sync.dma_start(
                    w_sc_raw[:].bitcast(I32)[32 * q + 4 * u : 32 * q + 4 * u + 4, :], ap[0].bitcast(I32)[4 * q : 4 * q + 4, :]
                )

        gm_16 = keep.tile([P, PACK], F32, name="gm_16")
        gn_inv = keep.tile([P, PACK], F32, name="gn_inv")
        gn_16 = keep.tile([P, PACK], F32, name="gn_16")
        gn_safe = keep.tile([P, PACK], F32, name="gn_safe", tag="tok_w%d" % B, align_bytes=64)
        nc.scalar.activation(gm_16[:], gm_sb[:], ACT.Copy, scale=SIXTEENTH)
        nc.scalar.activation(gn_16[:], gn_sb[:], ACT.Copy, scale=SIXTEENTH)
        nc.vector.scalar_tensor_tensor(gn_safe[:], gn_sb[:], 0.0, gn_sb[:], ALU.is_equal, ALU.add)
        nc.vector.reciprocal(gn_inv[:], gn_safe[:])

        a_n1 = keep.tile([P, PACK, S], F32, name="a_n1")
        tanh_n2 = keep.tile([P, PACK, S], F32, name="tanh_n2")
        b_n3 = keep.tile([P, PACK, S], F32, name="b_n3")
        st2 = keep.tile([P, PACK, ST2_WINDOW], F32, name="st2", align_bytes=64)
        st2_n4 = keep.tile([P, PACK, S], F32, name="st2_n4")
        nc.gpsimd.memset(st2[:, :, S:], 0.0)

        def copy_a(t):
            if t < A_ON_VECTOR:
                nc.vector.tensor_scalar(a_win[t][:, :S], a_banks[t][:], gn_16[:, t : t + 1], None, ALU.mult)
            else:
                nc.scalar.activation(a_win[t][:, :S], a_banks[t][:], ACT.Copy, scale=gn_16[:, t : t + 1])

        def make_st(t):
            nc.vector.tensor_tensor(st[:, t, :], a_win[t][:, :S], a_n1[:, t, :], ALU.add)

        def copy_b(t):
            nc.scalar.activation(b_win[t][:, :S], b_banks[t][:], ACT.Copy, scale=gm_16[:, t : t + 1])

        st = keep.tile([P, PACK, S], F32, name="st")
        w_sc = keep.tile([P, N], U8, name="w_sc", align_bytes=64)
        copy_b(0)
        for t in range(PACK):
            if t + 1 < PACK:
                copy_b(t + 1)
            nc.scalar.activation(b_n3[:, t, :], b_win[t][:].indirect(n3_l[:]), ACT.Copy)
            nc.vector.scalar_tensor_tensor(st2[:, t, :S], b_n3[:, t, :], 0.5, b_win[t][:, :S], ALU.mult, ALU.add)
            if t < A_ON_VECTOR:
                copy_a(t)
            nc.vector.tensor_copy(st2_n4[:, t, :], st2[:, t, :].indirect(n4_l[:]))
        for t in range(PACK):
            if A_ON_VECTOR <= t + 1 < PACK:
                copy_a(t + 1)
            nc.scalar.activation(a_n1[:, t, :], a_win[t][:].indirect(n1_l[:]), ACT.Copy)

        def mx_tiles(name, tag):
            rounded = keep.tile([P, S, PACK], BF16, name=name + "_bf", tag=tag, align_bytes=64)
            codes = keep.tile([P, S], U32, name=name + "_w", align_bytes=64)
            scales = keep.tile([P, S], U8, name=name + "_sc", align_bytes=64)
            return rounded, codes, scales

        def combine_and_quantize(dst, left, right, op, cols):
            rounded, codes, scales = dst
            nc.vector.tensor_tensor(
                by_column(rounded[:, cols, :]), by_row_tile(left[:, :, cols]), by_row_tile(right[:, :, cols]), op
            )
            nc.vector.quantize_mx(
                out=codes[:, cols].bitcast(FP8X4), scales=scales[:, cols], in_=rounded[:, cols, :].rearrange("p j t -> p (j t)")
            )

        z2_mx = mx_tiles("z2", "z2_bf")
        for t in range(PACK // 2):
            make_st(t)
        combine_and_quantize(z2_mx, st2, st2_n4, ALU.subtract, slice(0, S))
        for t in range(PACK // 2, PACK):
            make_st(t)
        deal(w_sc[:], w_sc_raw[:], 16)
        for u in (W1, W2):
            deal(w_w[:, u, :], w_raw[:, N * u : N * (u + 1)], 4)
        z_mx = mx_tiles("z", "x_sc")
        for t in range(PACK):
            nc.scalar.activation(a_win[t][:, :S], st[:, t, :], ACT.Tanh, scale=gn_inv[:, t : t + 1])
        halves = [slice(half * S // 2, (half + 1) * S // 2) for half in range(2)]
        for cols in halves:
            entries = slice(cols.start // GROUP, cols.stop // GROUP)
            for t in range(PACK):
                nc.scalar.activation(tanh_n2[:, t, cols], a_win[t][:].indirect(n2_l[:, entries]), ACT.Copy)
            combine_and_quantize(z_mx, st, tanh_n2, ALU.mult, cols)

        h = keep.tile([P, PACK, S], F32, name="h")
        ex = keep.tile([P, PACK, S], F32, name="ex")
        for left_by, cols in zip((B, A), halves):
            h_banks = [
                psum.tile([P, S // 2], F32, name="h%d%d" % (left_by, t), tag="bank%d%d" % (left_by, t)) for t in range(PACK)
            ]
            for u, (rounded, codes, scales) in ((W2, z2_mx), (W1, z_mx)):
                for t in range(PACK):
                    outs = slice(P * t, P * (t + 1))
                    nc.tensor.matmul_mx(
                        out=h_banks[t][:], lhsT=w_w[:, u, outs].bitcast(FP8X4), lhsT_scale=w_sc[4 * u :, outs],
                        rhs=codes[:, cols].bitcast(FP8X4), rhs_scale=scales[:, cols], start=(u == W2), stop=(u == W1),
                    )
            for t in range(PACK):
                nc.scalar.activation(a_win[t][:, cols], h_banks[t][:], ACT.Exp)
                nc.vector.tensor_copy(h[:, t, cols], h_banks[t][:])
        for t in range(PACK):
            nc.vector.tensor_copy(ex[:, t, :], a_win[t][:, :S])

        out_sc = keep.tile([P, S], U8, name="out_sc", align_bytes=64)
        out_rows = out_0.rearrange("(p t) j -> p t j", t=PACK)
        out_words = words_hbm(out_1)
        chunks = S // CHUNK
        for c in range(chunks):
            cols = slice(CHUNK * c, CHUNK * (c + 1))
            entries = slice(cols.start * MEMBERS // GROUP, cols.stop * MEMBERS // GROUP)
            ms = ring.tile([P, PACK, CHUNK], F32, name="ms")
            total = ring.tile([P, PACK, CHUNK], F32, name="total")
            logs = ring.tile([P, PACK, CHUNK], F32, name="logs")
            res = ring.tile([P, PACK, CHUNK], F32, name="res", bufs=chunks)
            parts = (slice(0, PACK - 1), slice(PACK - 1, PACK)) if c == chunks - 1 else (slice(0, PACK),)
            for part in parts:
                for t in range(part.start, part.stop):
                    mb = ring.tile([P, CHUNK, MEMBERS], F32, name="mb", bufs=PACK)
                    nc.scalar.activation(mb[:].rearrange("p j m -> p (j m)"), a_win[t][:].indirect(n5_l[:, entries]), ACT.Copy)
                    nc.vector.tensor_reduce(ms[:, t, :], mb[:], AXIS.X, ALU.add)
                nc.vector.tensor_tensor(total[:, part, :], ms[:, part, :], ex[:, part, cols], ALU.add)
                nc.scalar.activation(logs[:, part, :], total[:, part, :], ACT.Ln)
                nc.vector.tensor_tensor(res[:, part, :], logs[:, part, :], h[:, part, cols], ALU.subtract)
            nc.sync.dma_start(out_rows[:, :, cols], res[:])
            res_bf = ring.tile([P, CHUNK, PACK], BF16, name="res_bf", align_bytes=64)
            nc.vector.tensor_copy(out=by_column(res_bf[:]), in_=by_row_tile(res[:]))
            out_w = ring.tile([P, CHUNK], U32, name="out_w", bufs=chunks, align_bytes=64)
            nc.vector.quantize_mx(out=out_w[:].bitcast(FP8X4), scales=out_sc[:, cols], in_=res_bf[:].rearrange("p j t -> p (j t)"))
            nc.sync.dma_start(out_words[:, cols], out_w[:].bitcast(I32))
        for q in range(QUADRANTS):
            queue = nc.scalar if q % 2 else nc.sync
            queue.dma_start(out_2[0].bitcast(I32)[4 * q : 4 * q + 4, :], out_sc[:].bitcast(I32)[32 * q : 32 * q + 4, :])
